import numpy as np
import ml_dtypes


def mxq(x, axis, fmt="e4m3"):
    dtype, down = {"e4m3": (ml_dtypes.float8_e4m3fn, 7), "e5m2": (ml_dtypes.float8_e5m2, 14)}[fmt]
    v = np.moveaxis(np.asarray(x, np.float32).astype(ml_dtypes.bfloat16).astype(np.float64), axis, -1)
    blocks = v.reshape(v.shape[:-1] + (-1, 32))
    amax = np.abs(blocks).max(-1, keepdims=True)
    byte = np.maximum(np.where(amax > 0, np.frexp(amax)[1] - 1 + 127, 0) - down, 1)
    scale = np.exp2(byte - 127.0)
    codes = (blocks / scale).astype(np.float32).astype(dtype).astype(np.float64)
    return np.moveaxis((codes * scale).reshape(v.shape), -1, axis)


WIDE = False


def mx_kscale(k):
    if not WIDE:
        return np.ones(k)
    levels = np.array([10, -10, 5, -5, 0])
    if k % 512:
        return np.exp2(np.random.permutation(np.resize(levels, k // 32))).repeat(32)
    a = np.empty((k // 512, 16))
    for p in range(k // 512):
        a[p, :8] = np.random.permutation(np.resize(levels, 8))
        for g in range(8):
            far = levels[np.abs(levels - a[p, g]) >= 10]
            a[p, g + 8] = far[np.random.randint(len(far))]
    return np.exp2(a.ravel()).repeat(32)


def f64(x):
    return np.asarray(x).astype(np.float64)


def striped(idx):
    return np.tile(idx.reshape(-1, 16).T, (8, 1)).astype(np.uint16)


def unstriped(offs):
    return offs[:16].T.reshape(-1).astype(np.int64)


def pack_weight(w):
    k, n = w.shape
    w = f64(np.asarray(w, np.float32).astype(ml_dtypes.bfloat16)).reshape(k // 32, 32, n)
    amax = np.abs(w).max(1)
    byte = np.clip(np.where(amax > 0, np.frexp(amax)[1] - 1 + 127 - 7, 1), 1, 254)
    scaled = (w * np.exp2(127.0 - byte)[:, None, :]).reshape(k, n).astype(np.float32)
    words = np.ascontiguousarray(scaled.reshape(k // 512, 128, 4, n).transpose(0, 1, 3, 2)).astype(ml_dtypes.float8_e4m3fn).view(np.uint8)
    return words, np.ascontiguousarray(byte.astype(np.uint8).reshape(k // 512, 16, n))


def unpack_weight(words, scales):
    g, p, n, _ = words.shape
    vals = np.ascontiguousarray(words).view(ml_dtypes.float8_e4m3fn).astype(np.float64) * np.repeat(np.exp2(scales.astype(np.float64) - 127.0), 8, axis=1)[..., None]
    return vals.transpose(0, 1, 3, 2).reshape(g * 512, n)


def gelu(v):
    return 0.5 * v * (1.0 + np.tanh(np.sqrt(2.0 / np.pi) * (v + 0.044715 * v**3)))


K, T, E, C, N = 2048, 768, 18, 128, 128
TOP = 3


def by_expert(wq, xq):
    return np.concatenate([wq[e].T @ xq[:, e * C:(e + 1) * C] for e in range(E)], axis=1)


def setup_inputs():
    n = np.random.standard_normal
    s = mx_kscale(K)[:, None]
    deal = np.repeat(np.arange(E), C).reshape(TOP, T)[:, np.random.permutation(T)]
    deal = np.take_along_axis(deal, np.argsort(np.random.rand(TOP, T), axis=0), axis=0)
    for _ in range(8):
        s_, t_ = np.random.permutation(T).reshape(2, -1); r = np.random.randint(TOP, size=T // 2); x, y = deal[r, s_].copy(), deal[r, t_].copy()
        ok = ~((deal[:, s_] == y).any(0) | (deal[:, t_] == x).any(0)); deal[r[ok], s_[ok]] = y[ok]; deal[r[ok], t_[ok]] = x[ok]
    order = np.lexsort((np.random.rand(TOP * T), deal.reshape(-1)))
    slot_token = order % T; pos = np.empty(TOP * T, np.int64); pos[order] = np.arange(TOP * T); pos = pos.reshape(TOP, T)
    g = np.random.uniform(0.5, 1.5, (TOP, T)); g = g / g.sum(0)
    packed = [pack_weight(m) for m in n((E, K, N)) / np.sqrt(K) / s[None]]
    w_slot = np.empty(E * C)
    for r in range(TOP): w_slot[pos[r]] = g[r]
    return {
        "xT": (n((K, T)) * s).astype(np.float32),
        "w_words": np.stack([m[0] for m in packed]),
        "w_scales": np.stack([m[1] for m in packed]),
        "b": (0.3 * n((N, E))).astype(np.float32),
        "gate": np.tile(w_slot, (K, 1)).astype(np.float32),
        "offs": striped(slot_token),
        "pos1": striped(pos[0]),
        "pos2": striped(pos[1]),
        "pos3": striped(pos[2]),
    }


def reference(xT, w_words, w_scales, b, gate, offs, pos1, pos2, pos3):
    idx = unstriped(offs)
    w = np.stack([unpack_weight(w_words[e], w_scales[e]) for e in range(E)])
    xq = mxq(f64(gate) * f64(xT)[:, idx], 0, "e4m3")
    y = by_expert(w, xq)
    y = gelu(y + np.repeat(f64(b), C, axis=1))
    return y[:, unstriped(pos1)] + y[:, unstriped(pos2)] + y[:, unstriped(pos3)]

@@ -1,0 +1,167 @@
+from contextlib import ExitStack
+
+import concourse.mybir as mybir
+
+K, T, E, C, N = 2048, 768, 18, 128, 128
+S = E * C
+P = 128
+PACK = 4
+PASSES = K // (P * PACK)
+
+F32 = mybir.dt.float32
+BF16 = mybir.dt.bfloat16
+U32 = mybir.dt.uint32
+I32 = mybir.dt.int32
+U16 = mybir.dt.uint16
+U8 = mybir.dt.uint8
+FP8X4 = mybir.dt.float8_e4m3fn_x4
+MULT = mybir.AluOpType.mult
+ADD = mybir.AluOpType.add
+GELU = mybir.ActivationFunctionType.Gelu_apprx_tanh
+
+FLOPS = 2 * K * N * S
+BYTES = 4 * K * T + E * K * N + E * K * N // 32 + 4 * N * E + 4 * S + 2 * P * (S + 3 * T) // 16 + 4 * N * T
+
+WIDE = 512
+W_GROUP = 6
+
+
+def chunks(widths):
+    starts = [sum(widths[:i]) for i in range(len(widths))]
+    return list(zip(starts, widths))
+
+
+def tile_moe_pre_lin_gelu_kernel(tc, xT, w_words, w_scales, b, gate, offs, pos1, pos2, pos3, out):
+    nc = tc.nc
+    with ExitStack() as ctx:
+        lists = ctx.enter_context(tc.tile_pool(name="lists", bufs=1))
+        keep = ctx.enter_context(tc.tile_pool(name="keep", bufs=1))
+        stage = ctx.enter_context(tc.tile_pool(name="stage", bufs=2))
+        psum = ctx.enter_context(tc.psum_pool(name="psum", bufs=8))
+
+        wsc = keep.tile([P, E * PASSES * N], U8, name="wsc", align_bytes=64)
+        nc.vector.memset(wsc[:].bitcast(I32), 0)
+
+        offs_t = lists.tile([P, S // 16], U16, name="offs_t")
+        nc.sync.dma_start(offs_t[:], offs)
+
+        gate_t = {}
+
+        def load_gate(s0):
+            w = min(WIDE, S - s0)
+            gate_t[s0] = keep.tile([P, w], F32, name="gate%d" % s0)
+            nc.sync.dma_start(gate_t[s0][:], gate[0:P, s0 : s0 + w])
+
+        x_t = {}
+
+        def load_x(a):
+            rows = xT[a * P * PACK : (a + 1) * P * PACK, :].rearrange("(p t) w -> p t w", t=PACK)
+            for t in range(PACK):
+                x_t[a, t] = keep.tile([P, T], F32, name="x%d_%d" % (a, t))
+                nc.sync.dma_start(x_t[a, t][:], rows[:, t, :])
+
+        load_gate(0)
+        load_x(0)
+        for s0 in range(WIDE, S, WIDE):
+            load_gate(s0)
+        for a in range(1, PASSES):
+            load_x(a)
+
+        sc_rows = w_scales.rearrange("e a (q r) n -> r q (e a) n", r=4)
+        for r in range(4):
+            nc.sync.dma_start(
+                wsc[r:P:32, :].bitcast(I32).rearrange("p (g n) -> p g n", n=N // 4),
+                sc_rows[r].bitcast(I32),
+            )
+        w_all = w_words.rearrange("e a p n r -> p (e a) (n r)")
+        w_t = []
+        for g in range(E // W_GROUP):
+            wt = keep.tile([P, W_GROUP * PASSES * N * PACK], U8, name="w%d" % g, align_bytes=64)
+            nc.sync.dma_start(
+                wt[:].bitcast(I32).rearrange("p (g n) -> p g n", n=N),
+                w_all[:, g * W_GROUP * PASSES : (g + 1) * W_GROUP * PASSES, :].bitcast(I32),
+            )
+            w_t.append(wt)
+        b_t = keep.tile([P, E], F32, name="b_t")
+        nc.sync.dma_start(b_t[:], b)
+        pos_t = []
+        for i, pos in enumerate((pos1, pos2, pos3)):
+            pt = lists.tile([P, T // 16], U16, name="pos%d" % i)
+            nc.sync.dma_start(pt[:], pos)
+            pos_t.append(pt)
+
+        y = keep.tile([P, S], F32, name="y")
+        codes = {}
+
+        def gather(a, s0, w):
+            g = stage.tile([P, PACK * w], F32, name="g", tag="g")
+            g0 = s0 - s0 % WIDE
+            for t in range(PACK):
+                nc.vector.tensor_tensor(
+                    g[:, t * w : (t + 1) * w],
+                    x_t[a, t][:].indirect(offs_t[:, s0 // 16 : (s0 + w) // 16]),
+                    gate_t[g0][:, s0 - g0 : s0 - g0 + w],
+                    MULT,
+                )
+            xb = stage.tile([P, PACK * w], BF16, name="xb", tag="xb", align_bytes=64)
+            nc.scalar.copy(
+                xb[:].rearrange("p (s t) -> p s t", t=PACK),
+                g[:].rearrange("p (t s) -> p s t", t=PACK),
+            )
+            return xb
+
+        def quantize(a, s0, w, xb):
+            cw = keep.tile([P, w], U32, name="cw%d_%d" % (a, s0), align_bytes=64)
+            cs = keep.tile([P, w], U8, name="cs%d_%d" % (a, s0), align_bytes=64)
+            nc.vector.quantize_mx(out=cw[:].bitcast(FP8X4), scales=cs[:], in_=xb[:])
+            for e in range(s0 // C, (s0 + w) // C):
+                c0 = e * C - s0
+                codes[a, e] = (cw[:, c0 : c0 + C], cs[:, c0 : c0 + C])
+            if a == PASSES - 1:
+                for e in range(s0 // C, (s0 + w) // C):
+                    expert(e)
+
+        def expert(e):
+            acc = psum.tile([N, C], F32, name="acc", tag="acc")
+            wt = w_t[e // W_GROUP]
+            for a in range(PASSES):
+                g = (e % W_GROUP) * PASSES + a
+                ge = e * PASSES + a
+                nc.tensor.matmul_mx(
+                    out=acc[:],
+                    lhsT=wt[:, g * N * PACK : (g + 1) * N * PACK].bitcast(FP8X4),
+                    lhsT_scale=wsc[:, ge * N : (ge + 1) * N],
+                    rhs=codes[a, e][0].bitcast(FP8X4),
+                    rhs_scale=codes[a, e][1],
+                    start=(a == 0),
+                    stop=(a == PASSES - 1),
+                )
+            nc.scalar.activation(y[:, e * C : (e + 1) * C], acc[:], GELU, bias=b_t[:, e : e + 1])
+
+        steps = []
+        for a in range(PASSES):
+            widths = [WIDE] * 4 + ([C, C] if a == PASSES - 1 else [2 * C])
+            steps.extend((a, s0, w) for s0, w in chunks(widths))
+        waiting = None
+        for a, s0, w in steps:
+            xb = gather(a, s0, w)
+            if waiting is not None:
+                quantize(*waiting)
+            waiting = (a, s0, w, xb)
+        quantize(*waiting)
+
+        half = T // 2
+        sums = []
+        for h in range(2):
+            first = keep.tile([P, half], F32, name="first%d" % h)
+            nc.vector.tensor_copy(first[:], y[:].indirect(pos_t[0][:, h * half // 16 : (h + 1) * half // 16]))
+            sums.append(first)
+        for r in (1, 2):
+            for h in range(2):
+                more = keep.tile([P, half], F32, name="more%d_%d" % (r, h))
+                nc.vector.tensor_tensor(
+                    more[:], y[:].indirect(pos_t[r][:, h * half // 16 : (h + 1) * half // 16]), sums[h][:], ADD
+                )
+                sums[h] = more
+                if r == 2:
+                    nc.sync.dma_start(out[:, h * half : (h + 1) * half], more[:])

@@ -1,6 +1,7 @@
 from contextlib import ExitStack
 
 import concourse.mybir as mybir
+from concourse.masks import make_identity
 
 K, T, E, C, N = 2048, 768, 18, 128, 128
 S = E * C
@@ -17,13 +18,16 @@ U8 = mybir.dt.uint8
 FP8X4 = mybir.dt.float8_e4m3fn_x4
 MULT = mybir.AluOpType.mult
 ADD = mybir.AluOpType.add
+COPY = mybir.ActivationFunctionType.Copy
 GELU = mybir.ActivationFunctionType.Gelu_apprx_tanh
 
 FLOPS = 2 * K * N * S
 BYTES = 4 * K * T + E * K * N + E * K * N // 32 + 4 * N * E + 4 * S + 2 * P * (S + 3 * T) // 16 + 4 * N * T
 
-WIDE = 512
+CHUNKS = (768, 768, 512, 256)
+SPARE = 16
 W_GROUP = 6
+DIRECT = 2 * C
 
 
 def chunks(widths):
@@ -36,8 +40,9 @@ def tile_moe_pre_lin_gelu_kernel(tc, xT, w_words, w_scales, b, gate, offs, pos1,
     with ExitStack() as ctx:
         lists = ctx.enter_context(tc.tile_pool(name="lists", bufs=1))
         keep = ctx.enter_context(tc.tile_pool(name="keep", bufs=1))
-        stage = ctx.enter_context(tc.tile_pool(name="stage", bufs=2))
-        psum = ctx.enter_context(tc.psum_pool(name="psum", bufs=8))
+        stage = ctx.enter_context(tc.tile_pool(name="stage", bufs=3))
+        quant = ctx.enter_context(tc.tile_pool(name="quant", bufs=2))
+        psum = ctx.enter_context(tc.psum_pool(name="psum", bufs=3))
 
         wsc = keep.tile([P, E * PASSES * N], U8, name="wsc", align_bytes=64)
         nc.vector.memset(wsc[:].bitcast(I32), 0)
@@ -45,27 +50,28 @@ def tile_moe_pre_lin_gelu_kernel(tc, xT, w_words, w_scales, b, gate, offs, pos1,
         offs_t = lists.tile([P, S // 16], U16, name="offs_t")
         nc.sync.dma_start(offs_t[:], offs)
 
-        gate_t = {}
-
-        def load_gate(s0):
-            w = min(WIDE, S - s0)
-            gate_t[s0] = keep.tile([P, w], F32, name="gate%d" % s0)
-            nc.sync.dma_start(gate_t[s0][:], gate[0:P, s0 : s0 + w])
-
         x_t = {}
 
         def load_x(a):
             rows = xT[a * P * PACK : (a + 1) * P * PACK, :].rearrange("(p t) w -> p t w", t=PACK)
             for t in range(PACK):
-                x_t[a, t] = keep.tile([P, T], F32, name="x%d_%d" % (a, t))
-                nc.sync.dma_start(x_t[a, t][:], rows[:, t, :])
+                x_t[a, t] = keep.tile([P, T + SPARE], F32, name="x%d_%d" % (a, t))
+                nc.sync.dma_start(x_t[a, t][:, 0:T], rows[:, t, :])
 
-        load_gate(0)
-        load_x(0)
-        for s0 in range(WIDE, S, WIDE):
-            load_gate(s0)
-        for a in range(1, PASSES):
+        ident = keep.tile([P, P], F32, name="ident")
+        make_identity(nc, ident[:])
+        gate_rows = keep.tile([P, C], F32, name="gate_rows")
+        nc.gpsimd.memset(gate_rows[:], 0.0)
+        nc.scalar.dma_start(gate_rows[0:E, :], gate[0, :].rearrange("(e c) -> e c", c=C))
+        gate_ps = psum.tile([P, P], F32, name="gate_ps", tag="acc")
+        nc.tensor.transpose(gate_ps[:], gate_rows[:], ident[:])
+        gate_col = keep.tile([C, E], F32, name="gate_col")
+        nc.scalar.copy(gate_col[:], gate_ps[:, 0:E])
+
+        for a in range(PASSES):
             load_x(a)
+        gate_last = keep.tile([P, DIRECT], F32, name="gate_last")
+        nc.sync.dma_start(gate_last[:], gate[0:P, S - DIRECT : S])
 
         sc_rows = w_scales.rearrange("e a (q r) n -> r q (e a) n", r=4)
         for r in range(4):
@@ -93,27 +99,59 @@ def tile_moe_pre_lin_gelu_kernel(tc, xT, w_words, w_scales, b, gate, offs, pos1,
         y = keep.tile([P, S], F32, name="y")
         codes = {}
 
-        def gather(a, s0, w):
+        def slots(s0, w):
+            return offs_t[:, s0 // 16 : (s0 + w) // 16]
+
+        def gather_turned(a, s0, w):
             g = stage.tile([P, PACK * w], F32, name="g", tag="g")
-            g0 = s0 - s0 % WIDE
+            for t in range(PACK):
+                nc.vector.tensor_copy(g[:, t * w : (t + 1) * w], x_t[a, t][:].indirect(slots(s0, w)))
+            xb = stage.tile([P, PACK * w], BF16, name="xb", tag="xb", align_bytes=64)
+            for j0 in range(0, w // C, 2):
+                back = psum.tile([P, 2 * 2 * C], F32, name="back", tag="back", bufs=2)
+                for j in (j0, j0 + 1):
+                    e = s0 // C + j
+                    turned = psum.tile([C, PACK * P], F32, name="turned", tag="turned")
+                    for t in range(PACK):
+                        nc.tensor.transpose(
+                            turned[:, t * P : (t + 1) * P], g[:, t * w + j * C : t * w + (j + 1) * C], ident[:]
+                        )
+                    gated = stage.tile([C, PACK * P], BF16, name="gated", tag="gated", bufs=4)
+                    nc.scalar.activation(
+                        gated[:].rearrange("s (u p v) -> s u p v", u=2, v=2),
+                        turned[:].rearrange("s (u v p) -> s u p v", u=2, v=2),
+                        COPY,
+                        scale=gate_col[:, e : e + 1],
+                    )
+                    words = gated[:].bitcast(F32)
+                    for u in range(2):
+                        col = ((j - j0) * 2 + u) * C
+                        nc.tensor.transpose(back[:, col : col + C], words[:, u * P : (u + 1) * P], ident[:])
+                nc.scalar.copy(
+                    xb[:, j0 * C * PACK : (j0 + 2) * C * PACK].bitcast(F32).rearrange("p (j s u) -> p j s u", j=2, u=2),
+                    back[:].rearrange("p (j u s) -> p j s u", j=2, u=2),
+                )
+            return xb
+
+        def gather_direct(a, s0, w, copy):
+            g = stage.tile([P, PACK * w], F32, name="g", tag="g")
+            g0 = s0 - (S - DIRECT)
             for t in range(PACK):
                 nc.vector.tensor_tensor(
-                    g[:, t * w : (t + 1) * w],
-                    x_t[a, t][:].indirect(offs_t[:, s0 // 16 : (s0 + w) // 16]),
-                    gate_t[g0][:, s0 - g0 : s0 - g0 + w],
-                    MULT,
+                    g[:, t * w : (t + 1) * w], x_t[a, t][:].indirect(slots(s0, w)), gate_last[:, g0 : g0 + w], MULT
                 )
             xb = stage.tile([P, PACK * w], BF16, name="xb", tag="xb", align_bytes=64)
-            nc.scalar.copy(
-                xb[:].rearrange("p (s t) -> p s t", t=PACK),
-                g[:].rearrange("p (t s) -> p s t", t=PACK),
-            )
+            copy(xb[:].rearrange("p (s t) -> p s t", t=PACK), g[:].rearrange("p (t s) -> p s t", t=PACK))
             return xb
 
         def quantize(a, s0, w, xb):
-            cw = keep.tile([P, w], U32, name="cw%d_%d" % (a, s0), align_bytes=64)
-            cs = keep.tile([P, w], U8, name="cs%d_%d" % (a, s0), align_bytes=64)
-            nc.vector.quantize_mx(out=cw[:].bitcast(FP8X4), scales=cs[:], in_=xb[:])
+            cw = quant.tile([P, w], U32, name="cw", tag="cw%d" % a, align_bytes=64)
+            cs = quant.tile([P, w], U8, name="cs", tag="cs%d" % a, align_bytes=64)
+            for c0 in range(0, w, 512):
+                c1 = min(w, c0 + 512)
+                nc.vector.quantize_mx(
+                    out=cw[:, c0:c1].bitcast(FP8X4), scales=cs[:, c0:c1], in_=xb[:, c0 * PACK : c1 * PACK]
+                )
             for e in range(s0 // C, (s0 + w) // C):
                 c0 = e * C - s0
                 codes[a, e] = (cw[:, c0 : c0 + C], cs[:, c0 : c0 + C])
@@ -138,16 +176,17 @@ def tile_moe_pre_lin_gelu_kernel(tc, xT, w_words, w_scales, b, gate, offs, pos1,
                 )
             nc.scalar.activation(y[:, e * C : (e + 1) * C], acc[:], GELU, bias=b_t[:, e : e + 1])
 
-        steps = []
-        for a in range(PASSES):
-            widths = [WIDE] * 4 + ([C, C] if a == PASSES - 1 else [2 * C])
-            steps.extend((a, s0, w) for s0, w in chunks(widths))
+        steps = [(a, s0, w) for s0, w in chunks(CHUNKS) for a in range(PASSES)]
         waiting = None
-        for a, s0, w in steps:
-            xb = gather(a, s0, w)
+        for a, s0, w in steps[:-1]:
+            xb = gather_turned(a, s0, w)
             if waiting is not None:
                 quantize(*waiting)
             waiting = (a, s0, w, xb)
+        for s0, copy in ((S - 2 * C, nc.scalar.copy), (S - C, nc.vector.tensor_copy)):
+            xb = gather_direct(PASSES - 1, s0, C, copy)
+            quantize(*waiting)
+            waiting = (PASSES - 1, s0, C, xb)
         quantize(*waiting)
 
         half = T // 2

@@ -1,7 +1,7 @@
+import math
 from contextlib import ExitStack
 
 import concourse.mybir as mybir
-from concourse.masks import make_identity
 
 K, T, E, C, N = 2048, 768, 18, 128, 128
 S = E * C
@@ -24,10 +24,11 @@ GELU = mybir.ActivationFunctionType.Gelu_apprx_tanh
 FLOPS = 2 * K * N * S
 BYTES = 4 * K * T + E * K * N + E * K * N // 32 + 4 * N * E + 4 * S + 2 * P * (S + 3 * T) // 16 + 4 * N * T
 
-CHUNKS = (768, 768, 512, 256)
+CHUNKS = (1024, 768, 512)
+LAST = (256, 128, 128)
 SPARE = 16
+FIRST = (128, 256, 640)
 W_GROUP = 6
-DIRECT = 2 * C
 
 
 def chunks(widths):
@@ -41,11 +42,10 @@ def tile_moe_pre_lin_gelu_kernel(tc, xT, w_words, w_scales, b, gate, offs, pos1,
         lists = ctx.enter_context(tc.tile_pool(name="lists", bufs=1))
         keep = ctx.enter_context(tc.tile_pool(name="keep", bufs=1))
         stage = ctx.enter_context(tc.tile_pool(name="stage", bufs=3))
-        quant = ctx.enter_context(tc.tile_pool(name="quant", bufs=2))
-        psum = ctx.enter_context(tc.psum_pool(name="psum", bufs=3))
+        quant = ctx.enter_context(tc.tile_pool(name="quant", bufs=4))
+        psum = ctx.enter_context(tc.psum_pool(name="psum", bufs=8))
 
         wsc = keep.tile([P, E * PASSES * N], U8, name="wsc", align_bytes=64)
-        nc.vector.memset(wsc[:].bitcast(I32), 0)
 
         offs_t = lists.tile([P, S // 16], U16, name="offs_t")
         nc.sync.dma_start(offs_t[:], offs)
@@ -55,23 +55,18 @@ def tile_moe_pre_lin_gelu_kernel(tc, xT, w_words, w_scales, b, gate, offs, pos1,
         def load_x(a):
             rows = xT[a * P * PACK : (a + 1) * P * PACK, :].rearrange("(p t) w -> p t w", t=PACK)
             for t in range(PACK):
-                x_t[a, t] = keep.tile([P, T + SPARE], F32, name="x%d_%d" % (a, t))
+                x_t[a, t] = keep.tile([P, CHUNKS[0] + SPARE], F32, name="x%d_%d" % (a, t))
                 nc.sync.dma_start(x_t[a, t][:, 0:T], rows[:, t, :])
+                if (a, t) == (0, 0):
+                    for c0, cw in chunks(FIRST)[1:]:
+                        nc.sync.dma_start(gate_t[:, c0 : c0 + cw], gate[0:P, c0 : c0 + cw])
 
-        ident = keep.tile([P, P], F32, name="ident")
-        make_identity(nc, ident[:])
-        gate_rows = keep.tile([P, C], F32, name="gate_rows")
-        nc.gpsimd.memset(gate_rows[:], 0.0)
-        nc.scalar.dma_start(gate_rows[0:E, :], gate[0, :].rearrange("(e c) -> e c", c=C))
-        gate_ps = psum.tile([P, P], F32, name="gate_ps", tag="acc")
-        nc.tensor.transpose(gate_ps[:], gate_rows[:], ident[:])
-        gate_col = keep.tile([C, E], F32, name="gate_col")
-        nc.scalar.copy(gate_col[:], gate_ps[:, 0:E])
-
+        nc.gpsimd.memset(wsc[:].bitcast(I32), 0)
+        gate_t = keep.tile([P, S], F32, name="gate_t")
+        nc.scalar.dma_start(gate_t[:, 0 : FIRST[0]], gate[0:P, 0 : FIRST[0]])
         for a in range(PASSES):
             load_x(a)
-        gate_last = keep.tile([P, DIRECT], F32, name="gate_last")
-        nc.sync.dma_start(gate_last[:], gate[0:P, S - DIRECT : S])
+        nc.sync.dma_start(gate_t[:, CHUNKS[0] : S], gate[0:P, CHUNKS[0] : S])
 
         sc_rows = w_scales.rearrange("e a (q r) n -> r q (e a) n", r=4)
         for r in range(4):
@@ -97,110 +92,84 @@ def tile_moe_pre_lin_gelu_kernel(tc, xT, w_words, w_scales, b, gate, offs, pos1,
             pos_t.append(pt)
 
         y = keep.tile([P, S], F32, name="y")
-        codes = {}
+        acc = {}
 
         def slots(s0, w):
             return offs_t[:, s0 // 16 : (s0 + w) // 16]
 
-        def gather_turned(a, s0, w):
-            g = stage.tile([P, PACK * w], F32, name="g", tag="g")
-            for t in range(PACK):
-                nc.vector.tensor_copy(g[:, t * w : (t + 1) * w], x_t[a, t][:].indirect(slots(s0, w)))
-            xb = stage.tile([P, PACK * w], BF16, name="xb", tag="xb", align_bytes=64)
-            for j0 in range(0, w // C, 2):
-                back = psum.tile([P, 2 * 2 * C], F32, name="back", tag="back", bufs=2)
-                for j in (j0, j0 + 1):
-                    e = s0 // C + j
-                    turned = psum.tile([C, PACK * P], F32, name="turned", tag="turned")
-                    for t in range(PACK):
-                        nc.tensor.transpose(
-                            turned[:, t * P : (t + 1) * P], g[:, t * w + j * C : t * w + (j + 1) * C], ident[:]
-                        )
-                    gated = stage.tile([C, PACK * P], BF16, name="gated", tag="gated", bufs=4)
-                    nc.scalar.activation(
-                        gated[:].rearrange("s (u p v) -> s u p v", u=2, v=2),
-                        turned[:].rearrange("s (u v p) -> s u p v", u=2, v=2),
-                        COPY,
-                        scale=gate_col[:, e : e + 1],
-                    )
-                    words = gated[:].bitcast(F32)
-                    for u in range(2):
-                        col = ((j - j0) * 2 + u) * C
-                        nc.tensor.transpose(back[:, col : col + C], words[:, u * P : (u + 1) * P], ident[:])
-                nc.scalar.copy(
-                    xb[:, j0 * C * PACK : (j0 + 2) * C * PACK].bitcast(F32).rearrange("p (j s u) -> p j s u", j=2, u=2),
-                    back[:].rearrange("p (j u s) -> p j s u", j=2, u=2),
-                )
-            return xb
-
         def gather_direct(a, s0, w, copy):
-            g = stage.tile([P, PACK * w], F32, name="g", tag="g")
-            g0 = s0 - (S - DIRECT)
+            g = stage.tile([P, PACK * w + PACK * w // 2], F32, name="g", tag="g", align_bytes=64)
             for t in range(PACK):
-                nc.vector.tensor_tensor(
-                    g[:, t * w : (t + 1) * w], x_t[a, t][:].indirect(slots(s0, w)), gate_last[:, g0 : g0 + w], MULT
-                )
-            xb = stage.tile([P, PACK * w], BF16, name="xb", tag="xb", align_bytes=64)
-            copy(xb[:].rearrange("p (s t) -> p s t", t=PACK), g[:].rearrange("p (t s) -> p s t", t=PACK))
+                cuts = FIRST if (a, s0, t) == (0, 0, 0) else (w,)
+                for c0, cw in chunks(cuts):
+                    nc.vector.tensor_tensor(
+                        g[:, t * w + c0 : t * w + c0 + cw],
+                        x_t[a, t][:].indirect(slots(s0 + c0, cw)),
+                        gate_t[:, s0 + c0 : s0 + c0 + cw],
+                        MULT,
+                    )
+            xb = g[:, PACK * w :].bitcast(BF16)
+            copy(xb.rearrange("p (s t) -> p s t", t=PACK), g[:, 0 : PACK * w].rearrange("p (t s) -> p s t", t=PACK))
             return xb
 
         def quantize(a, s0, w, xb):
-            cw = quant.tile([P, w], U32, name="cw", tag="cw%d" % a, align_bytes=64)
-            cs = quant.tile([P, w], U8, name="cs", tag="cs%d" % a, align_bytes=64)
-            for c0 in range(0, w, 512):
-                c1 = min(w, c0 + 512)
+            cw = quant.tile([P, w], U32, name="cw", tag="cw", align_bytes=64)
+            cs = quant.tile([P, w], U8, name="cs", tag="cs", align_bytes=64)
+            wide = 1 << int(math.log2(w))
+            for c0, c1 in ((0, wide), (wide, w))[: 1 if wide == w else 2]:
                 nc.vector.quantize_mx(
                     out=cw[:, c0:c1].bitcast(FP8X4), scales=cs[:, c0:c1], in_=xb[:, c0 * PACK : c1 * PACK]
                 )
             for e in range(s0 // C, (s0 + w) // C):
                 c0 = e * C - s0
-                codes[a, e] = (cw[:, c0 : c0 + C], cs[:, c0 : c0 + C])
+                multiply(a, e, cw[:, c0 : c0 + C], cs[:, c0 : c0 + C])
+
+        def multiply(a, e, words, scales):
+            if a == 0:
+                acc[e] = psum.tile([N, C], F32, name="acc", tag="acc")
+            g = (e % W_GROUP) * PASSES + a
+            ge = e * PASSES + a
+            nc.tensor.matmul_mx(
+                out=acc[e][:],
+                lhsT=w_t[e // W_GROUP][:, g * N * PACK : (g + 1) * N * PACK].bitcast(FP8X4),
+                lhsT_scale=wsc[:, ge * N : (ge + 1) * N],
+                rhs=words.bitcast(FP8X4),
+                rhs_scale=scales,
+                start=(a == 0),
+                stop=(a == PASSES - 1),
+            )
             if a == PASSES - 1:
-                for e in range(s0 // C, (s0 + w) // C):
-                    expert(e)
+                nc.scalar.activation(y[:, e * C : (e + 1) * C], acc[e][:], GELU, bias=b_t[:, e : e + 1])
 
-        def expert(e):
-            acc = psum.tile([N, C], F32, name="acc", tag="acc")
-            wt = w_t[e // W_GROUP]
-            for a in range(PASSES):
-                g = (e % W_GROUP) * PASSES + a
-                ge = e * PASSES + a
-                nc.tensor.matmul_mx(
-                    out=acc[:],
-                    lhsT=wt[:, g * N * PACK : (g + 1) * N * PACK].bitcast(FP8X4),
-                    lhsT_scale=wsc[:, ge * N : (ge + 1) * N],
-                    rhs=codes[a, e][0].bitcast(FP8X4),
-                    rhs_scale=codes[a, e][1],
-                    start=(a == 0),
-                    stop=(a == PASSES - 1),
-                )
-            nc.scalar.activation(y[:, e * C : (e + 1) * C], acc[:], GELU, bias=b_t[:, e : e + 1])
-
-        steps = [(a, s0, w) for s0, w in chunks(CHUNKS) for a in range(PASSES)]
+        steps = [(a, s0, w) for s0, w in chunks(CHUNKS) for a in range(PASSES)][:-1]
+        steps.extend((PASSES - 1, S - CHUNKS[-1] + s0, w) for s0, w in chunks(LAST))
         waiting = None
-        for a, s0, w in steps[:-1]:
-            xb = gather_turned(a, s0, w)
+        for a, s0, w in steps:
+            xb = gather_direct(a, s0, w, nc.vector.tensor_copy if (a, s0) == (PASSES - 1, S - C) else nc.scalar.copy)
             if waiting is not None:
                 quantize(*waiting)
             waiting = (a, s0, w, xb)
-        for s0, copy in ((S - 2 * C, nc.scalar.copy), (S - C, nc.vector.tensor_copy)):
-            xb = gather_direct(PASSES - 1, s0, C, copy)
-            quantize(*waiting)
-            waiting = (PASSES - 1, s0, C, xb)
         quantize(*waiting)
 
+        room = stage.tile([P, 3 * T], F32, name="room", tag="g", align_bytes=64)
         half = T // 2
         sums = []
         for h in range(2):
-            first = keep.tile([P, half], F32, name="first%d" % h)
-            nc.vector.tensor_copy(first[:], y[:].indirect(pos_t[0][:, h * half // 16 : (h + 1) * half // 16]))
+            first = room[:, h * half : (h + 1) * half]
+            nc.vector.tensor_copy(first, y[:].indirect(pos_t[0][:, h * half // 16 : (h + 1) * half // 16]))
             sums.append(first)
-        for r in (1, 2):
-            for h in range(2):
-                more = keep.tile([P, half], F32, name="more%d_%d" % (r, h))
-                nc.vector.tensor_tensor(
-                    more[:], y[:].indirect(pos_t[r][:, h * half // 16 : (h + 1) * half // 16]), sums[h][:], ADD
-                )
-                sums[h] = more
-                if r == 2:
-                    nc.sync.dma_start(out[:, h * half : (h + 1) * half], more[:])
+        for h in range(2):
+            more = room[:, T + h * half : T + (h + 1) * half]
+            nc.vector.tensor_tensor(
+                more, y[:].indirect(pos_t[1][:, h * half // 16 : (h + 1) * half // 16]), sums[h], ADD
+            )
+            sums[h] = more
+        for t0, w in chunks((half, 2 * C, C)):
+            total = room[:, 2 * T + t0 : 2 * T + t0 + w]
+            nc.vector.tensor_tensor(
+                total,
+                y[:].indirect(pos_t[2][:, t0 // 16 : (t0 + w) // 16]),
+                sums[t0 // half][:, t0 % half : t0 % half + w],
+                ADD,
+            )
+            nc.sync.dma_start(out[:, t0 : t0 + w], total)

@@ -24,8 +24,8 @@ GELU = mybir.ActivationFunctionType.Gelu_apprx_tanh
 FLOPS = 2 * K * N * S
 BYTES = 4 * K * T + E * K * N + E * K * N // 32 + 4 * N * E + 4 * S + 2 * P * (S + 3 * T) // 16 + 4 * N * T
 
-CHUNKS = (1024, 768, 512)
-LAST = (256, 128, 128)
+CHUNKS = (1024, 1024, 256)
+LAST = (128, 128)
 SPARE = 16
 FIRST = (128, 256, 640)
 W_GROUP = 6
@@ -109,7 +109,10 @@ def tile_moe_pre_lin_gelu_kernel(tc, xT, w_words, w_scales, b, gate, offs, pos1,
                         MULT,
                     )
             xb = g[:, PACK * w :].bitcast(BF16)
-            copy(xb.rearrange("p (s t) -> p s t", t=PACK), g[:, 0 : PACK * w].rearrange("p (t s) -> p s t", t=PACK))
+            copy(
+                xb.rearrange("p (c i t) -> p c t i", i=4, t=PACK),
+                g[:, 0 : PACK * w].rearrange("p (t c i) -> p c t i", i=4, t=PACK),
+            )
             return xb
 
         def quantize(a, s0, w, xb):

import math
from contextlib import ExitStack

import concourse.mybir as mybir

K, T, E, C, N = 2048, 768, 18, 128, 128
S = E * C
P = 128
PACK = 4
PASSES = K // (P * PACK)

F32 = mybir.dt.float32
BF16 = mybir.dt.bfloat16
U32 = mybir.dt.uint32
I32 = mybir.dt.int32
U16 = mybir.dt.uint16
U8 = mybir.dt.uint8
FP8X4 = mybir.dt.float8_e4m3fn_x4
MULT = mybir.AluOpType.mult
ADD = mybir.AluOpType.add
COPY = mybir.ActivationFunctionType.Copy
GELU = mybir.ActivationFunctionType.Gelu_apprx_tanh

FLOPS = 2 * K * N * S
BYTES = 4 * K * T + E * K * N + E * K * N // 32 + 4 * N * E + 4 * S + 2 * P * (S + 3 * T) // 16 + 4 * N * T

CHUNKS = (1024, 1024, 256)
LAST = (128, 128)
SPARE = 16
FIRST = (128, 256, 640)
W_GROUP = 6


def chunks(widths):
    starts = [sum(widths[:i]) for i in range(len(widths))]
    return list(zip(starts, widths))


def tile_moe_pre_lin_gelu_kernel(tc, xT, w_words, w_scales, b, gate, offs, pos1, pos2, pos3, out):
    nc = tc.nc
    with ExitStack() as ctx:
        lists = ctx.enter_context(tc.tile_pool(name="lists", bufs=1))
        keep = ctx.enter_context(tc.tile_pool(name="keep", bufs=1))
        stage = ctx.enter_context(tc.tile_pool(name="stage", bufs=3))
        quant = ctx.enter_context(tc.tile_pool(name="quant", bufs=4))
        psum = ctx.enter_context(tc.psum_pool(name="psum", bufs=8))

        wsc = keep.tile([P, E * PASSES * N], U8, name="wsc", align_bytes=64)

        offs_t = lists.tile([P, S // 16], U16, name="offs_t")
        nc.sync.dma_start(offs_t[:], offs)

        x_t = {}

        def load_x(a):
            rows = xT[a * P * PACK : (a + 1) * P * PACK, :].rearrange("(p t) w -> p t w", t=PACK)
            for t in range(PACK):
                x_t[a, t] = keep.tile([P, CHUNKS[0] + SPARE], F32, name="x%d_%d" % (a, t))
                nc.sync.dma_start(x_t[a, t][:, 0:T], rows[:, t, :])
                if (a, t) == (0, 0):
                    for c0, cw in chunks(FIRST)[1:]:
                        nc.sync.dma_start(gate_t[:, c0 : c0 + cw], gate[0:P, c0 : c0 + cw])

        nc.gpsimd.memset(wsc[:].bitcast(I32), 0)
        gate_t = keep.tile([P, S], F32, name="gate_t")
        nc.scalar.dma_start(gate_t[:, 0 : FIRST[0]], gate[0:P, 0 : FIRST[0]])
        for a in range(PASSES):
            load_x(a)
        nc.sync.dma_start(gate_t[:, CHUNKS[0] : S], gate[0:P, CHUNKS[0] : S])

        sc_rows = w_scales.rearrange("e a (q r) n -> r q (e a) n", r=4)
        for r in range(4):
            nc.sync.dma_start(
                wsc[r:P:32, :].bitcast(I32).rearrange("p (g n) -> p g n", n=N // 4),
                sc_rows[r].bitcast(I32),
            )
        w_all = w_words.rearrange("e a p n r -> p (e a) (n r)")
        w_t = []
        for g in range(E // W_GROUP):
            wt = keep.tile([P, W_GROUP * PASSES * N * PACK], U8, name="w%d" % g, align_bytes=64)
            nc.sync.dma_start(
                wt[:].bitcast(I32).rearrange("p (g n) -> p g n", n=N),
                w_all[:, g * W_GROUP * PASSES : (g + 1) * W_GROUP * PASSES, :].bitcast(I32),
            )
            w_t.append(wt)
        b_t = keep.tile([P, E], F32, name="b_t")
        nc.sync.dma_start(b_t[:], b)
        pos_t = []
        for i, pos in enumerate((pos1, pos2, pos3)):
            pt = lists.tile([P, T // 16], U16, name="pos%d" % i)
            nc.sync.dma_start(pt[:], pos)
            pos_t.append(pt)

        y = keep.tile([P, S], F32, name="y")
        acc = {}

        def slots(s0, w):
            return offs_t[:, s0 // 16 : (s0 + w) // 16]

        def gather_direct(a, s0, w, copy):
            g = stage.tile([P, PACK * w + PACK * w // 2], F32, name="g", tag="g", align_bytes=64)
            for t in range(PACK):
                cuts = FIRST if (a, s0, t) == (0, 0, 0) else (w,)
                for c0, cw in chunks(cuts):
                    nc.vector.tensor_tensor(
                        g[:, t * w + c0 : t * w + c0 + cw],
                        x_t[a, t][:].indirect(slots(s0 + c0, cw)),
                        gate_t[:, s0 + c0 : s0 + c0 + cw],
                        MULT,
                    )
            xb = g[:, PACK * w :].bitcast(BF16)
            copy(
                xb.rearrange("p (c i t) -> p c t i", i=4, t=PACK),
                g[:, 0 : PACK * w].rearrange("p (t c i) -> p c t i", i=4, t=PACK),
            )
            return xb

        def quantize(a, s0, w, xb):
            cw = quant.tile([P, w], U32, name="cw", tag="cw", align_bytes=64)
            cs = quant.tile([P, w], U8, name="cs", tag="cs", align_bytes=64)
            wide = 1 << int(math.log2(w))
            for c0, c1 in ((0, wide), (wide, w))[: 1 if wide == w else 2]:
                nc.vector.quantize_mx(
                    out=cw[:, c0:c1].bitcast(FP8X4), scales=cs[:, c0:c1], in_=xb[:, c0 * PACK : c1 * PACK]
                )
            for e in range(s0 // C, (s0 + w) // C):
                c0 = e * C - s0
                multiply(a, e, cw[:, c0 : c0 + C], cs[:, c0 : c0 + C])

        def multiply(a, e, words, scales):
            if a == 0:
                acc[e] = psum.tile([N, C], F32, name="acc", tag="acc")
            g = (e % W_GROUP) * PASSES + a
            ge = e * PASSES + a
            nc.tensor.matmul_mx(
                out=acc[e][:],
                lhsT=w_t[e // W_GROUP][:, g * N * PACK : (g + 1) * N * PACK].bitcast(FP8X4),
                lhsT_scale=wsc[:, ge * N : (ge + 1) * N],
                rhs=words.bitcast(FP8X4),
                rhs_scale=scales,
                start=(a == 0),
                stop=(a == PASSES - 1),
            )
            if a == PASSES - 1:
                nc.scalar.activation(y[:, e * C : (e + 1) * C], acc[e][:], GELU, bias=b_t[:, e : e + 1])

        steps = [(a, s0, w) for s0, w in chunks(CHUNKS) for a in range(PASSES)][:-1]
        steps.extend((PASSES - 1, S - CHUNKS[-1] + s0, w) for s0, w in chunks(LAST))
        waiting = None
        for a, s0, w in steps:
            xb = gather_direct(a, s0, w, nc.vector.tensor_copy if (a, s0) == (PASSES - 1, S - C) else nc.scalar.copy)
            if waiting is not None:
                quantize(*waiting)
            waiting = (a, s0, w, xb)
        quantize(*waiting)

        room = stage.tile([P, 3 * T], F32, name="room", tag="g", align_bytes=64)
        half = T // 2
        sums = []
        for h in range(2):
            first = room[:, h * half : (h + 1) * half]
            nc.vector.tensor_copy(first, y[:].indirect(pos_t[0][:, h * half // 16 : (h + 1) * half // 16]))
            sums.append(first)
        for h in range(2):
            more = room[:, T + h * half : T + (h + 1) * half]
            nc.vector.tensor_tensor(
                more, y[:].indirect(pos_t[1][:, h * half // 16 : (h + 1) * half // 16]), sums[h], ADD
            )
            sums[h] = more
        for t0, w in chunks((half, 2 * C, C)):
            total = room[:, 2 * T + t0 : 2 * T + t0 + w]
            nc.vector.tensor_tensor(
                total,
                y[:].indirect(pos_t[2][:, t0 // 16 : (t0 + w) // 16]),
                sums[t0 // half][:, t0 % half : t0 % half + w],
                ADD,
            )
            nc.sync.dma_start(out[:, t0 : t0 + w], total)
